import numpy as np
import ml_dtypes


def mxq(x, axis, fmt="e4m3"):
    dtype, down = {"e4m3": (ml_dtypes.float8_e4m3fn, 7), "e5m2": (ml_dtypes.float8_e5m2, 14)}[fmt]
    v = np.moveaxis(np.asarray(x, np.float32).astype(ml_dtypes.bfloat16).astype(np.float64), axis, -1)
    blocks = v.reshape(v.shape[:-1] + (-1, 32))
    amax = np.abs(blocks).max(-1, keepdims=True)
    byte = np.maximum(np.where(amax > 0, np.frexp(amax)[1] - 1 + 127, 0) - down, 1)
    scale = np.exp2(byte - 127.0)
    codes = (blocks / scale).astype(np.float32).astype(dtype).astype(np.float64)
    return np.moveaxis((codes * scale).reshape(v.shape), -1, axis)


WIDE = False


def mx_kscale(k):
    if not WIDE:
        return np.ones(k)
    levels = np.array([10, -10, 5, -5, 0])
    if k % 512:
        return np.exp2(np.random.permutation(np.resize(levels, k // 32))).repeat(32)
    a = np.empty((k // 512, 16))
    for p in range(k // 512):
        a[p, :8] = np.random.permutation(np.resize(levels, 8))
        for g in range(8):
            far = levels[np.abs(levels - a[p, g]) >= 10]
            a[p, g + 8] = far[np.random.randint(len(far))]
    return np.exp2(a.ravel()).repeat(32)


def f64(x):
    return np.asarray(x).astype(np.float64)


def striped(idx):
    return np.tile(idx.reshape(-1, 16).T, (8, 1)).astype(np.uint16)


def unstriped(offs):
    return offs[:16].T.reshape(-1).astype(np.int64)


def pack_weight(w):
    k, n = w.shape
    w = f64(np.asarray(w, np.float32).astype(ml_dtypes.bfloat16)).reshape(k // 32, 32, n)
    amax = np.abs(w).max(1)
    byte = np.clip(np.where(amax > 0, np.frexp(amax)[1] - 1 + 127 - 7, 1), 1, 254)
    scaled = (w * np.exp2(127.0 - byte)[:, None, :]).reshape(k, n).astype(np.float32)
    words = np.ascontiguousarray(scaled.reshape(k // 512, 128, 4, n).transpose(0, 1, 3, 2)).astype(ml_dtypes.float8_e4m3fn).view(np.uint8)
    return words, np.ascontiguousarray(byte.astype(np.uint8).reshape(k // 512, 16, n))


def unpack_weight(words, scales):
    g, p, n, _ = words.shape
    vals = np.ascontiguousarray(words).view(ml_dtypes.float8_e4m3fn).astype(np.float64) * np.repeat(np.exp2(scales.astype(np.float64) - 127.0), 8, axis=1)[..., None]
    return vals.transpose(0, 1, 3, 2).reshape(g * 512, n)


K, T, S, N, U, D, V = 1024, 1024, 512, 256, 512, 4, 128
P = 2 ** 7


def setup_inputs():
    n = np.random.standard_normal
    s = mx_kscale(K)[:, None]
    packed_xT = pack_weight(n((K, T)) * s)
    return {
        "x_words": packed_xT[0],
        "x_scales": packed_xT[1],
        "w1": (n((K, N)) / np.sqrt(K) / s).astype(np.float32),
        "att": (np.tile(np.random.uniform(0.2, 1.0, U), (P, 1))).astype(np.float32),
        "hand": (np.tile(np.random.uniform(0.1, 0.6, U), (P, 1))).astype(np.float32),
        "pred": (np.random.uniform(0.2, 1.5, (N, V))).astype(np.float32),
        "offs": striped(np.random.permutation(T)[:S]),
        "eats": striped(np.random.randint(0, S, U)),
    }


def reference(x_words, x_scales, w1, att, hand, pred, offs, eats):
    xq = unpack_weight(x_words, x_scales)[:, unstriped(offs)]
    y = mxq(f64(w1), 0, "e4m3").T @ xq
    prey = np.exp(0.5 * y)
    enc = prey[:, unstriped(eats)] * f64(att)[:1]
    gh = enc * f64(hand)[:1]
    busy = gh.reshape(len(gh), -1, D).sum(axis=2) + 1.0
    eat = enc / np.repeat(busy, D, axis=1)
    return f64(pred) * (0.4 * (eat.reshape(len(eat), -1, D).sum(axis=2)) - 0.3)

@@ -1,0 +1,178 @@
+from contextlib import ExitStack
+
+import concourse.mybir as mybir
+
+K, T, S, N, U, D, V = 1024, 1024, 512, 256, 512, 4, 128
+FLOPS = 2 * K * N * S
+
+F32 = mybir.dt.float32
+BF16 = mybir.dt.bfloat16
+I32 = mybir.dt.int32
+U32 = mybir.dt.uint32
+U16 = mybir.dt.uint16
+U8 = mybir.dt.uint8
+FP8X4 = mybir.dt.float8_e4m3fn_x4
+ALU = mybir.AluOpType
+ACT = mybir.ActivationFunctionType
+
+P = 128
+PACK = 4
+K_PASS = P * PACK
+PASSES = K // K_PASS
+BLOCKS = N // P
+EXP_WINDOW = 2048
+CUTS = 2
+
+
+def tile_picked_yholl_pred_p_kernel(
+    tc, x_words, x_scales, w1, att, hand, pred, offs, eats, out
+):
+    nc = tc.nc
+    with ExitStack() as ctx:
+        keep = ctx.enter_context(tc.tile_pool(name="keep", bufs=1))
+        psum = ctx.enter_context(tc.psum_pool(name="psum", bufs=1))
+
+        offs_sb = keep.tile([P, S // 16], U16, name="offs_sb")
+        eats_sb = keep.tile([P, U // 16], U16, name="eats_sb")
+        table_scales = keep.tile([P, T], U8, name="table_scales", align_bytes=64)
+        table_words = [keep.tile([P, T], U32, name="table_words%d" % g, align_bytes=64) for g in range(PASSES)]
+        w_raw = [[keep.tile([P, PACK, P], F32, name="w_raw%d_%d" % (b, g)) for g in range(PASSES)] for b in range(BLOCKS)]
+        att_sb = keep.tile([P, U], F32, name="att_sb")
+        hand_sb = keep.tile([P, U], F32, name="hand_sb")
+        pred_sb = keep.tile([P, BLOCKS, V], F32, name="pred_sb")
+        warm = keep.tile([P, 2], F32, name="warm")
+        half_y = keep.tile([P, EXP_WINDOW], F32, name="half_y")
+
+        nc.vector.memset(table_scales[:].bitcast(I32), 0)
+        nc.vector.memset(warm[:, 0:1], 1.0)
+        nc.vector.memset(half_y[:, S:], 0.0)
+        nc.scalar.activation(warm[:, 1:2], warm[:, 0:1], ACT.Exp)
+
+        def load_words(g):
+            nc.sync.dma_start(table_words[g][:].bitcast(I32), x_words[g].rearrange("p c r -> p (c r)").bitcast(I32))
+
+        def load_w(b, g):
+            rows = w1[g * K_PASS : (g + 1) * K_PASS, b * P : (b + 1) * P]
+            nc.sync.dma_start(w_raw[b][g][:], rows.rearrange("(p j) m -> p j m", j=PACK))
+
+        nc.sync.dma_start(offs_sb[:], offs)
+        load_w(0, 0)
+        for q in range(4):
+            nc.sync.dma_start(
+                table_scales[32 * q : 32 * q + 4 * PASSES, :].bitcast(I32),
+                x_scales[:, 4 * q : 4 * q + 4, :].bitcast(I32),
+            )
+        load_words(0)
+        load_w(0, 1)
+        load_words(1)
+        load_w(1, 0)
+        load_w(1, 1)
+        nc.sync.dma_start(eats_sb[:], eats)
+        nc.sync.dma_start(att_sb[:], att)
+        nc.sync.dma_start(hand_sb[:], hand)
+        nc.sync.dma_start(pred_sb[:], pred.rearrange("(b p) v -> p b v", p=P))
+
+        picked_scales = keep.tile([P, S], U8, name="picked_scales", align_bytes=64)
+        picked_words = [
+            [keep.tile([P, S // CUTS], U32, name="picked_words%d_%d" % (g, c), align_bytes=64) for c in range(CUTS)]
+            for g in range(PASSES)
+        ]
+        w_words = {}
+        w_scales = {}
+        width = S // CUTS
+
+        def pick_words(g, c):
+            entries = offs_sb[:, c * width // 16 : (c + 1) * width // 16]
+            nc.vector.tensor_copy(picked_words[g][c][:], table_words[g][:].indirect(entries))
+
+        def quantize_w(b, g):
+            grouped = keep.tile([P, P, PACK], BF16, name="grouped%d_%d" % (b, g), align_bytes=64)
+            dst = grouped[:].rearrange("p (c i) t -> p c t i", i=4)
+            src = w_raw[b][g][:].rearrange("p t (c i) -> p c t i", i=4)
+            if (b, g) == (BLOCKS - 1, PASSES - 1):
+                nc.vector.tensor_copy(dst, src)
+            else:
+                nc.scalar.copy(dst, src)
+            w_words[b, g] = keep.tile([P, P], U32, name="w_words%d_%d" % (b, g), align_bytes=64)
+            w_scales[b, g] = keep.tile([P, P], U8, name="w_scales%d_%d" % (b, g), align_bytes=64)
+            nc.vector.quantize_mx(
+                out=w_words[b, g][:].bitcast(FP8X4),
+                scales=w_scales[b, g][:],
+                in_=grouped[:].rearrange("p c t -> p (c t)"),
+            )
+
+        y = [[psum.tile([P, S], F32, name="y%d_%d" % (b, c)) for c in range(CUTS)] for b in range(BLOCKS)]
+
+        def multiply(b, g, c):
+            nc.tensor.matmul_mx(
+                out=y[b][c][:, 0:width],
+                lhsT=w_words[b, g][:].bitcast(FP8X4),
+                lhsT_scale=w_scales[b, g][:],
+                rhs=picked_words[g][c][:].bitcast(FP8X4),
+                rhs_scale=picked_scales[4 * g : P, c * width : (c + 1) * width],
+                start=(g == 0),
+                stop=(g == PASSES - 1),
+            )
+
+        nc.vector.tensor_copy(picked_scales[:], table_scales[:].indirect(offs_sb[:]))
+        for g in range(PASSES):
+            if g == 0:
+                for c in range(CUTS):
+                    pick_words(g, c)
+                quantize_w(0, g)
+            else:
+                quantize_w(0, g)
+                for c in range(CUTS):
+                    pick_words(g, c)
+            for c in range(CUTS):
+                multiply(0, g, c)
+        prey0 = keep.tile([P, S], F32, name="prey0")
+        for c in range(CUTS):
+            nc.scalar.activation(prey0[:, c * width : (c + 1) * width], y[0][c][:, 0:width], ACT.Exp, scale=0.5)
+        for g in range(PASSES):
+            quantize_w(1, g)
+            for c in range(CUTS):
+                multiply(1, g, c)
+        for c in range(CUTS):
+            nc.scalar.activation(half_y[:, c * width : (c + 1) * width], y[1][c][:, 0:width], ACT.Copy, scale=0.5)
+        eaten1 = keep.tile([P, U], F32, name="eaten1")
+        nc.scalar.activation(eaten1[:], half_y[:].indirect(eats_sb[:]), ACT.Exp)
+        nc.scalar.activation(warm[:, 1:2], eaten1[:, 0:1], ACT.Abs_reciprocal_sqrt)
+
+        def group_sums(terms, label):
+            pairs = keep.tile([P, V, 2], F32, name="pairs_" + label)
+            sums = keep.tile([P, V], F32, name="sums_" + label)
+            four = terms[:].rearrange("p (v d) -> p v d", d=D)
+            nc.vector.tensor_tensor(pairs[:], four[:, :, 0:2], four[:, :, 2:4], ALU.add)
+            nc.vector.tensor_tensor(sums[:], pairs[:, :, 0], pairs[:, :, 1], ALU.add)
+            return sums
+
+        links = U // CUTS
+        for b in range(BLOCKS):
+            enc = keep.tile([P, U], F32, name="enc%d" % b)
+            gh = keep.tile([P, U], F32, name="gh%d" % b)
+            for c in range(CUTS):
+                cols = slice(c * links, (c + 1) * links)
+                if b == 0:
+                    found = prey0[:].indirect(eats_sb[:, c * links // 16 : (c + 1) * links // 16])
+                else:
+                    found = eaten1[:, cols]
+                nc.vector.tensor_tensor(enc[:, cols], found, att_sb[:, cols], ALU.mult)
+            for c in range(CUTS):
+                cols = slice(c * links, (c + 1) * links)
+                nc.vector.tensor_tensor(gh[:, cols], enc[:, cols], hand_sb[:, cols], ALU.mult)
+            handled = group_sums(gh, "gh%d" % b)
+            root = keep.tile([P, V], F32, name="root%d" % b)
+            inv = keep.tile([P, V], F32, name="inv%d" % b)
+            sign = keep.tile([P, V], F32, name="sign%d" % b)
+            nc.scalar.activation(sign[:], handled[:], ACT.Sign, bias=1.0)
+            nc.scalar.activation(root[:], handled[:], ACT.Abs_reciprocal_sqrt, bias=1.0)
+            nc.scalar.activation(inv[:], root[:], ACT.Square)
+            met = group_sums(enc, "enc%d" % b)
+            gain = keep.tile([P, V], F32, name="gain%d" % b)
+            nc.vector.scalar_tensor_tensor(gain[:], met[:], 0.4, sign[:], ALU.mult, ALU.mult)
+            rate = keep.tile([P, V], F32, name="rate%d" % b)
+            nc.vector.tensor_tensor(rate[:], gain[:], inv[:], ALU.mult)
+            res = keep.tile([P, V], F32, name="res%d" % b)
+            nc.vector.scalar_tensor_tensor(res[:], rate[:], 0.3, pred_sb[:, b, :], ALU.subtract, ALU.mult)
+            nc.sync.dma_start(out[b * P : (b + 1) * P, :], res[:])

@@ -1,6 +1,7 @@
 from contextlib import ExitStack
 
 import concourse.mybir as mybir
+from concourse.masks import make_identity
 
 K, T, S, N, U, D, V = 1024, 1024, 512, 256, 512, 4, 128
 FLOPS = 2 * K * N * S
@@ -20,7 +21,6 @@ PACK = 4
 K_PASS = P * PACK
 PASSES = K // K_PASS
 BLOCKS = N // P
-EXP_WINDOW = 2048
 CUTS = 2
 
 
@@ -41,12 +41,12 @@ def tile_picked_yholl_pred_p_kernel(
         hand_sb = keep.tile([P, U], F32, name="hand_sb")
         pred_sb = keep.tile([P, BLOCKS, V], F32, name="pred_sb")
         warm = keep.tile([P, 2], F32, name="warm")
-        half_y = keep.tile([P, EXP_WINDOW], F32, name="half_y")
+        identity = keep.tile([P, P], F32, name="identity")
+        make_identity(nc, identity[:])
 
+        landed_scales = keep.tile([P, T], U8, name="landed_scales", align_bytes=64)
         nc.vector.memset(table_scales[:].bitcast(I32), 0)
         nc.vector.memset(warm[:, 0:1], 1.0)
-        nc.vector.memset(half_y[:, S:], 0.0)
-        nc.scalar.activation(warm[:, 1:2], warm[:, 0:1], ACT.Exp)
 
         def load_words(g):
             nc.sync.dma_start(table_words[g][:].bitcast(I32), x_words[g].rearrange("p c r -> p (c r)").bitcast(I32))
@@ -55,14 +55,14 @@ def tile_picked_yholl_pred_p_kernel(
             rows = w1[g * K_PASS : (g + 1) * K_PASS, b * P : (b + 1) * P]
             nc.sync.dma_start(w_raw[b][g][:], rows.rearrange("(p j) m -> p j m", j=PACK))
 
-        nc.sync.dma_start(offs_sb[:], offs)
-        load_w(0, 0)
+        live = [slice(32 * q, 32 * q + 4 * PASSES) for q in range(4)]
         for q in range(4):
-            nc.sync.dma_start(
-                table_scales[32 * q : 32 * q + 4 * PASSES, :].bitcast(I32),
-                x_scales[:, 4 * q : 4 * q + 4, :].bitcast(I32),
-            )
+            queue = nc.sync if q % 2 == 0 else nc.scalar
+            queue.dma_start(landed_scales[live[q], :].bitcast(I32), x_scales[:, 4 * q : 4 * q + 4, :].bitcast(I32))
+        nc.scalar.activation(warm[:, 1:2], warm[:, 0:1], ACT.Exp)
+        nc.sync.dma_start(offs_sb[:], offs)
         load_words(0)
+        load_w(0, 0)
         load_w(0, 1)
         load_words(1)
         load_w(1, 0)
@@ -73,17 +73,14 @@ def tile_picked_yholl_pred_p_kernel(
         nc.sync.dma_start(pred_sb[:], pred.rearrange("(b p) v -> p b v", p=P))
 
         picked_scales = keep.tile([P, S], U8, name="picked_scales", align_bytes=64)
-        picked_words = [
-            [keep.tile([P, S // CUTS], U32, name="picked_words%d_%d" % (g, c), align_bytes=64) for c in range(CUTS)]
-            for g in range(PASSES)
-        ]
+        picked_words = [keep.tile([P, S], U32, name="picked_words%d" % g, align_bytes=64) for g in range(PASSES)]
         w_words = {}
         w_scales = {}
         width = S // CUTS
 
-        def pick_words(g, c):
-            entries = offs_sb[:, c * width // 16 : (c + 1) * width // 16]
-            nc.vector.tensor_copy(picked_words[g][c][:], table_words[g][:].indirect(entries))
+        def pick_words(g, lo, hi):
+            entries = offs_sb[:, lo // 16 : hi // 16]
+            nc.vector.tensor_copy(picked_words[g][:, lo:hi], table_words[g][:].indirect(entries))
 
         def quantize_w(b, g):
             grouped = keep.tile([P, P, PACK], BF16, name="grouped%d_%d" % (b, g), align_bytes=64)
@@ -108,71 +105,98 @@ def tile_picked_yholl_pred_p_kernel(
                 out=y[b][c][:, 0:width],
                 lhsT=w_words[b, g][:].bitcast(FP8X4),
                 lhsT_scale=w_scales[b, g][:],
-                rhs=picked_words[g][c][:].bitcast(FP8X4),
+                rhs=picked_words[g][:, c * width : (c + 1) * width].bitcast(FP8X4),
                 rhs_scale=picked_scales[4 * g : P, c * width : (c + 1) * width],
                 start=(g == 0),
                 stop=(g == PASSES - 1),
             )
 
+        for q in range(4):
+            nc.vector.tensor_copy(table_scales[live[q], :].bitcast(I32), landed_scales[live[q], :].bitcast(I32))
         nc.vector.tensor_copy(picked_scales[:], table_scales[:].indirect(offs_sb[:]))
         for g in range(PASSES):
             if g == 0:
-                for c in range(CUTS):
-                    pick_words(g, c)
+                pick_words(g, 0, S)
                 quantize_w(0, g)
             else:
                 quantize_w(0, g)
                 for c in range(CUTS):
-                    pick_words(g, c)
+                    pick_words(g, c * width, (c + 1) * width)
             for c in range(CUTS):
                 multiply(0, g, c)
-        prey0 = keep.tile([P, S], F32, name="prey0")
-        for c in range(CUTS):
-            nc.scalar.activation(prey0[:, c * width : (c + 1) * width], y[0][c][:, 0:width], ACT.Exp, scale=0.5)
+        prey = [keep.tile([P, S], F32, name="prey%d" % b) for b in range(BLOCKS)]
+
+        def exp_block(b):
+            for c in range(CUTS):
+                nc.scalar.activation(prey[b][:, c * width : (c + 1) * width], y[b][c][:, 0:width], ACT.Exp, scale=0.5)
+
+        exp_block(0)
         for g in range(PASSES):
             quantize_w(1, g)
             for c in range(CUTS):
                 multiply(1, g, c)
-        for c in range(CUTS):
-            nc.scalar.activation(half_y[:, c * width : (c + 1) * width], y[1][c][:, 0:width], ACT.Copy, scale=0.5)
-        eaten1 = keep.tile([P, U], F32, name="eaten1")
-        nc.scalar.activation(eaten1[:], half_y[:].indirect(eats_sb[:]), ACT.Exp)
-        nc.scalar.activation(warm[:, 1:2], eaten1[:, 0:1], ACT.Abs_reciprocal_sqrt)
-
-        def group_sums(terms, label):
-            pairs = keep.tile([P, V, 2], F32, name="pairs_" + label)
-            sums = keep.tile([P, V], F32, name="sums_" + label)
-            four = terms[:].rearrange("p (v d) -> p v d", d=D)
-            nc.vector.tensor_tensor(pairs[:], four[:, :, 0:2], four[:, :, 2:4], ALU.add)
-            nc.vector.tensor_tensor(sums[:], pairs[:, :, 0], pairs[:, :, 1], ALU.add)
-            return sums
+        exp_block(1)
+        nc.scalar.activation(warm[:, 1:2], prey[1][:, S - 1 : S], ACT.Abs_reciprocal_sqrt)
 
         links = U // CUTS
-        for b in range(BLOCKS):
+
+        def link_terms(b):
             enc = keep.tile([P, U], F32, name="enc%d" % b)
             gh = keep.tile([P, U], F32, name="gh%d" % b)
             for c in range(CUTS):
                 cols = slice(c * links, (c + 1) * links)
-                if b == 0:
-                    found = prey0[:].indirect(eats_sb[:, c * links // 16 : (c + 1) * links // 16])
-                else:
-                    found = eaten1[:, cols]
+                found = prey[b][:].indirect(eats_sb[:, c * links // 16 : (c + 1) * links // 16])
                 nc.vector.tensor_tensor(enc[:, cols], found, att_sb[:, cols], ALU.mult)
             for c in range(CUTS):
                 cols = slice(c * links, (c + 1) * links)
                 nc.vector.tensor_tensor(gh[:, cols], enc[:, cols], hand_sb[:, cols], ALU.mult)
-            handled = group_sums(gh, "gh%d" % b)
-            root = keep.tile([P, V], F32, name="root%d" % b)
-            inv = keep.tile([P, V], F32, name="inv%d" % b)
-            sign = keep.tile([P, V], F32, name="sign%d" % b)
-            nc.scalar.activation(sign[:], handled[:], ACT.Sign, bias=1.0)
-            nc.scalar.activation(root[:], handled[:], ACT.Abs_reciprocal_sqrt, bias=1.0)
+            return enc, gh
+
+        def turned_sums(terms, label):
+            acc = psum.tile([P, S], F32, name="turned_" + label)
+            four = terms[:].rearrange("p (v d) -> p d v", d=D)
+            for d in range(D):
+                nc.tensor.matmul(
+                    acc[:, 0:P], lhsT=four[:, d, :], rhs=identity[:], start=(d == 0), stop=(d == D - 1), is_transpose=True
+                )
+            return acc[:, 0:P]
+
+        def growth(met, handled, density, label):
+            root = keep.tile([P, V], F32, name="root" + label)
+            inv = keep.tile([P, V], F32, name="inv" + label)
+            sign = keep.tile([P, V], F32, name="sign" + label)
+            nc.scalar.activation(sign[:], handled, ACT.Sign, bias=1.0)
+            nc.scalar.activation(root[:], handled, ACT.Abs_reciprocal_sqrt, bias=1.0)
             nc.scalar.activation(inv[:], root[:], ACT.Square)
-            met = group_sums(enc, "enc%d" % b)
-            gain = keep.tile([P, V], F32, name="gain%d" % b)
-            nc.vector.scalar_tensor_tensor(gain[:], met[:], 0.4, sign[:], ALU.mult, ALU.mult)
-            rate = keep.tile([P, V], F32, name="rate%d" % b)
+            gain = keep.tile([P, V], F32, name="gain" + label)
+            nc.vector.scalar_tensor_tensor(gain[:], met, 0.4, sign[:], ALU.mult, ALU.mult)
+            rate = keep.tile([P, V], F32, name="rate" + label)
             nc.vector.tensor_tensor(rate[:], gain[:], inv[:], ALU.mult)
-            res = keep.tile([P, V], F32, name="res%d" % b)
-            nc.vector.scalar_tensor_tensor(res[:], rate[:], 0.3, pred_sb[:, b, :], ALU.subtract, ALU.mult)
-            nc.sync.dma_start(out[b * P : (b + 1) * P, :], res[:])
+            res = keep.tile([P, V], F32, name="res" + label)
+            nc.vector.scalar_tensor_tensor(res[:], rate[:], 0.3, density, ALU.subtract, ALU.mult)
+            return res
+
+        enc0, gh0 = link_terms(0)
+        met0 = turned_sums(enc0, "enc")
+        handled0 = turned_sums(gh0, "gh")
+        pred_turned = psum.tile([P, S], F32, name="pred_turned")
+        nc.tensor.transpose(pred_turned[:, 0:P], pred_sb[:, 0, :], identity[:])
+
+        enc1, gh1 = link_terms(1)
+        res_turned = growth(met0, handled0, pred_turned[:, 0:P], "0")
+        back = psum.tile([P, S], F32, name="back")
+        nc.tensor.transpose(back[:, 0:P], res_turned[:], identity[:])
+        res0 = keep.tile([P, V], F32, name="res0_sb")
+        nc.scalar.copy(res0[:], back[:, 0:P])
+        nc.sync.dma_start(out[0:P, :], res0[:])
+
+        pairs = [keep.tile([P, V, 2], F32, name="pairs%d" % i) for i in range(2)]
+        sums = [keep.tile([P, V], F32, name="sums%d" % i) for i in range(2)]
+        for i, terms in enumerate((gh1, enc1)):
+            four = terms[:].rearrange("p (v d) -> p v d", d=D)
+            nc.vector.tensor_tensor(pairs[i][:], four[:, :, 0:2], four[:, :, 2:4], ALU.add)
+        for i in range(2):
+            nc.vector.tensor_tensor(sums[i][:], pairs[i][:, :, 0], pairs[i][:, :, 1], ALU.add)
+
+        res1 = growth(sums[1][:], sums[0][:], pred_sb[:, 1, :], "1")
+        nc.sync.dma_start(out[P : 2 * P, :], res1[:])

@@ -22,6 +22,7 @@ K_PASS = P * PACK
 PASSES = K // K_PASS
 BLOCKS = N // P
 CUTS = 2
+PIECES = (((0, 256), (256, 384), (384, 512)), ((0, 256), (256, 512)))
 
 
 def tile_picked_yholl_pred_p_kernel(
@@ -76,7 +77,6 @@ def tile_picked_yholl_pred_p_kernel(
         picked_words = [keep.tile([P, S], U32, name="picked_words%d" % g, align_bytes=64) for g in range(PASSES)]
         w_words = {}
         w_scales = {}
-        width = S // CUTS
 
         def pick_words(g, lo, hi):
             entries = offs_sb[:, lo // 16 : hi // 16]
@@ -98,44 +98,38 @@ def tile_picked_yholl_pred_p_kernel(
                 in_=grouped[:].rearrange("p c t -> p (c t)"),
             )
 
-        y = [[psum.tile([P, S], F32, name="y%d_%d" % (b, c)) for c in range(CUTS)] for b in range(BLOCKS)]
-
-        def multiply(b, g, c):
+        def multiply(acc, b, g, lo, hi):
             nc.tensor.matmul_mx(
-                out=y[b][c][:, 0:width],
+                out=acc[:, 0 : hi - lo],
                 lhsT=w_words[b, g][:].bitcast(FP8X4),
                 lhsT_scale=w_scales[b, g][:],
-                rhs=picked_words[g][:, c * width : (c + 1) * width].bitcast(FP8X4),
-                rhs_scale=picked_scales[4 * g : P, c * width : (c + 1) * width],
+                rhs=picked_words[g][:, lo:hi].bitcast(FP8X4),
+                rhs_scale=picked_scales[4 * g : P, lo:hi],
                 start=(g == 0),
                 stop=(g == PASSES - 1),
             )
 
+        prey = [keep.tile([P, S], F32, name="prey%d" % b) for b in range(BLOCKS)]
+        y = [[psum.tile([P, S], F32, name="y%d_%d" % (b, c)) for c in range(len(PIECES[b]))] for b in range(BLOCKS)]
+
         for q in range(4):
             nc.vector.tensor_copy(table_scales[live[q], :].bitcast(I32), landed_scales[live[q], :].bitcast(I32))
         nc.vector.tensor_copy(picked_scales[:], table_scales[:].indirect(offs_sb[:]))
-        for g in range(PASSES):
-            if g == 0:
-                pick_words(g, 0, S)
-                quantize_w(0, g)
-            else:
-                quantize_w(0, g)
-                for c in range(CUTS):
-                    pick_words(g, c * width, (c + 1) * width)
-            for c in range(CUTS):
-                multiply(0, g, c)
-        prey = [keep.tile([P, S], F32, name="prey%d" % b) for b in range(BLOCKS)]
-
-        def exp_block(b):
-            for c in range(CUTS):
-                nc.scalar.activation(prey[b][:, c * width : (c + 1) * width], y[b][c][:, 0:width], ACT.Exp, scale=0.5)
-
-        exp_block(0)
+        pick_words(0, 0, S)
+        quantize_w(0, 0)
+        for acc, (lo, hi) in zip(y[0], PIECES[0]):
+            multiply(acc, 0, 0, lo, hi)
+        quantize_w(0, 1)
+        for acc, (lo, hi) in zip(y[0], PIECES[0]):
+            pick_words(1, lo, hi)
+            multiply(acc, 0, 1, lo, hi)
+            nc.scalar.activation(prey[0][:, lo:hi], acc[:, 0 : hi - lo], ACT.Exp, scale=0.5)
         for g in range(PASSES):
             quantize_w(1, g)
-            for c in range(CUTS):
-                multiply(1, g, c)
-        exp_block(1)
+            for acc, (lo, hi) in zip(y[1], PIECES[1]):
+                multiply(acc, 1, g, lo, hi)
+        for acc, (lo, hi) in zip(y[1], PIECES[1]):
+            nc.scalar.activation(prey[1][:, lo:hi], acc[:, 0 : hi - lo], ACT.Exp, scale=0.5)
         nc.scalar.activation(warm[:, 1:2], prey[1][:, S - 1 : S], ACT.Abs_reciprocal_sqrt)
 
         links = U // CUTS
@@ -184,7 +178,7 @@ def tile_picked_yholl_pred_p_kernel(
 
         enc1, gh1 = link_terms(1)
         res_turned = growth(met0, handled0, pred_turned[:, 0:P], "0")
-        back = psum.tile([P, S], F32, name="back")
+        back = psum.tile([P, S], F32, name="back", tag="y0_0")
         nc.tensor.transpose(back[:, 0:P], res_turned[:], identity[:])
         res0 = keep.tile([P, V], F32, name="res0_sb")
         nc.scalar.copy(res0[:], back[:, 0:P])

from contextlib import ExitStack

import concourse.mybir as mybir
from concourse.masks import make_identity

K, T, S, N, U, D, V = 1024, 1024, 512, 256, 512, 4, 128
FLOPS = 2 * K * N * S

F32 = mybir.dt.float32
BF16 = mybir.dt.bfloat16
I32 = mybir.dt.int32
U32 = mybir.dt.uint32
U16 = mybir.dt.uint16
U8 = mybir.dt.uint8
FP8X4 = mybir.dt.float8_e4m3fn_x4
ALU = mybir.AluOpType
ACT = mybir.ActivationFunctionType

P = 128
PACK = 4
K_PASS = P * PACK
PASSES = K // K_PASS
BLOCKS = N // P
CUTS = 2
PIECES = (((0, 256), (256, 384), (384, 512)), ((0, 256), (256, 512)))


def tile_picked_yholl_pred_p_kernel(
    tc, x_words, x_scales, w1, att, hand, pred, offs, eats, out
):
    nc = tc.nc
    with ExitStack() as ctx:
        keep = ctx.enter_context(tc.tile_pool(name="keep", bufs=1))
        psum = ctx.enter_context(tc.psum_pool(name="psum", bufs=1))

        offs_sb = keep.tile([P, S // 16], U16, name="offs_sb")
        eats_sb = keep.tile([P, U // 16], U16, name="eats_sb")
        table_scales = keep.tile([P, T], U8, name="table_scales", align_bytes=64)
        table_words = [keep.tile([P, T], U32, name="table_words%d" % g, align_bytes=64) for g in range(PASSES)]
        w_raw = [[keep.tile([P, PACK, P], F32, name="w_raw%d_%d" % (b, g)) for g in range(PASSES)] for b in range(BLOCKS)]
        att_sb = keep.tile([P, U], F32, name="att_sb")
        hand_sb = keep.tile([P, U], F32, name="hand_sb")
        pred_sb = keep.tile([P, BLOCKS, V], F32, name="pred_sb")
        warm = keep.tile([P, 2], F32, name="warm")
        identity = keep.tile([P, P], F32, name="identity")
        make_identity(nc, identity[:])

        landed_scales = keep.tile([P, T], U8, name="landed_scales", align_bytes=64)
        nc.vector.memset(table_scales[:].bitcast(I32), 0)
        nc.vector.memset(warm[:, 0:1], 1.0)

        def load_words(g):
            nc.sync.dma_start(table_words[g][:].bitcast(I32), x_words[g].rearrange("p c r -> p (c r)").bitcast(I32))

        def load_w(b, g):
            rows = w1[g * K_PASS : (g + 1) * K_PASS, b * P : (b + 1) * P]
            nc.sync.dma_start(w_raw[b][g][:], rows.rearrange("(p j) m -> p j m", j=PACK))

        live = [slice(32 * q, 32 * q + 4 * PASSES) for q in range(4)]
        for q in range(4):
            queue = nc.sync if q % 2 == 0 else nc.scalar
            queue.dma_start(landed_scales[live[q], :].bitcast(I32), x_scales[:, 4 * q : 4 * q + 4, :].bitcast(I32))
        nc.scalar.activation(warm[:, 1:2], warm[:, 0:1], ACT.Exp)
        nc.sync.dma_start(offs_sb[:], offs)
        load_words(0)
        load_w(0, 0)
        load_w(0, 1)
        load_words(1)
        load_w(1, 0)
        load_w(1, 1)
        nc.sync.dma_start(eats_sb[:], eats)
        nc.sync.dma_start(att_sb[:], att)
        nc.sync.dma_start(hand_sb[:], hand)
        nc.sync.dma_start(pred_sb[:], pred.rearrange("(b p) v -> p b v", p=P))

        picked_scales = keep.tile([P, S], U8, name="picked_scales", align_bytes=64)
        picked_words = [keep.tile([P, S], U32, name="picked_words%d" % g, align_bytes=64) for g in range(PASSES)]
        w_words = {}
        w_scales = {}

        def pick_words(g, lo, hi):
            entries = offs_sb[:, lo // 16 : hi // 16]
            nc.vector.tensor_copy(picked_words[g][:, lo:hi], table_words[g][:].indirect(entries))

        def quantize_w(b, g):
            grouped = keep.tile([P, P, PACK], BF16, name="grouped%d_%d" % (b, g), align_bytes=64)
            dst = grouped[:].rearrange("p (c i) t -> p c t i", i=4)
            src = w_raw[b][g][:].rearrange("p t (c i) -> p c t i", i=4)
            if (b, g) == (BLOCKS - 1, PASSES - 1):
                nc.vector.tensor_copy(dst, src)
            else:
                nc.scalar.copy(dst, src)
            w_words[b, g] = keep.tile([P, P], U32, name="w_words%d_%d" % (b, g), align_bytes=64)
            w_scales[b, g] = keep.tile([P, P], U8, name="w_scales%d_%d" % (b, g), align_bytes=64)
            nc.vector.quantize_mx(
                out=w_words[b, g][:].bitcast(FP8X4),
                scales=w_scales[b, g][:],
                in_=grouped[:].rearrange("p c t -> p (c t)"),
            )

        def multiply(acc, b, g, lo, hi):
            nc.tensor.matmul_mx(
                out=acc[:, 0 : hi - lo],
                lhsT=w_words[b, g][:].bitcast(FP8X4),
                lhsT_scale=w_scales[b, g][:],
                rhs=picked_words[g][:, lo:hi].bitcast(FP8X4),
                rhs_scale=picked_scales[4 * g : P, lo:hi],
                start=(g == 0),
                stop=(g == PASSES - 1),
            )

        prey = [keep.tile([P, S], F32, name="prey%d" % b) for b in range(BLOCKS)]
        y = [[psum.tile([P, S], F32, name="y%d_%d" % (b, c)) for c in range(len(PIECES[b]))] for b in range(BLOCKS)]

        for q in range(4):
            nc.vector.tensor_copy(table_scales[live[q], :].bitcast(I32), landed_scales[live[q], :].bitcast(I32))
        nc.vector.tensor_copy(picked_scales[:], table_scales[:].indirect(offs_sb[:]))
        pick_words(0, 0, S)
        quantize_w(0, 0)
        for acc, (lo, hi) in zip(y[0], PIECES[0]):
            multiply(acc, 0, 0, lo, hi)
        quantize_w(0, 1)
        for acc, (lo, hi) in zip(y[0], PIECES[0]):
            pick_words(1, lo, hi)
            multiply(acc, 0, 1, lo, hi)
            nc.scalar.activation(prey[0][:, lo:hi], acc[:, 0 : hi - lo], ACT.Exp, scale=0.5)
        for g in range(PASSES):
            quantize_w(1, g)
            for acc, (lo, hi) in zip(y[1], PIECES[1]):
                multiply(acc, 1, g, lo, hi)
        for acc, (lo, hi) in zip(y[1], PIECES[1]):
            nc.scalar.activation(prey[1][:, lo:hi], acc[:, 0 : hi - lo], ACT.Exp, scale=0.5)
        nc.scalar.activation(warm[:, 1:2], prey[1][:, S - 1 : S], ACT.Abs_reciprocal_sqrt)

        links = U // CUTS

        def link_terms(b):
            enc = keep.tile([P, U], F32, name="enc%d" % b)
            gh = keep.tile([P, U], F32, name="gh%d" % b)
            for c in range(CUTS):
                cols = slice(c * links, (c + 1) * links)
                found = prey[b][:].indirect(eats_sb[:, c * links // 16 : (c + 1) * links // 16])
                nc.vector.tensor_tensor(enc[:, cols], found, att_sb[:, cols], ALU.mult)
            for c in range(CUTS):
                cols = slice(c * links, (c + 1) * links)
                nc.vector.tensor_tensor(gh[:, cols], enc[:, cols], hand_sb[:, cols], ALU.mult)
            return enc, gh

        def turned_sums(terms, label):
            acc = psum.tile([P, S], F32, name="turned_" + label)
            four = terms[:].rearrange("p (v d) -> p d v", d=D)
            for d in range(D):
                nc.tensor.matmul(
                    acc[:, 0:P], lhsT=four[:, d, :], rhs=identity[:], start=(d == 0), stop=(d == D - 1), is_transpose=True
                )
            return acc[:, 0:P]

        def growth(met, handled, density, label):
            root = keep.tile([P, V], F32, name="root" + label)
            inv = keep.tile([P, V], F32, name="inv" + label)
            sign = keep.tile([P, V], F32, name="sign" + label)
            nc.scalar.activation(sign[:], handled, ACT.Sign, bias=1.0)
            nc.scalar.activation(root[:], handled, ACT.Abs_reciprocal_sqrt, bias=1.0)
            nc.scalar.activation(inv[:], root[:], ACT.Square)
            gain = keep.tile([P, V], F32, name="gain" + label)
            nc.vector.scalar_tensor_tensor(gain[:], met, 0.4, sign[:], ALU.mult, ALU.mult)
            rate = keep.tile([P, V], F32, name="rate" + label)
            nc.vector.tensor_tensor(rate[:], gain[:], inv[:], ALU.mult)
            res = keep.tile([P, V], F32, name="res" + label)
            nc.vector.scalar_tensor_tensor(res[:], rate[:], 0.3, density, ALU.subtract, ALU.mult)
            return res

        enc0, gh0 = link_terms(0)
        met0 = turned_sums(enc0, "enc")
        handled0 = turned_sums(gh0, "gh")
        pred_turned = psum.tile([P, S], F32, name="pred_turned")
        nc.tensor.transpose(pred_turned[:, 0:P], pred_sb[:, 0, :], identity[:])

        enc1, gh1 = link_terms(1)
        res_turned = growth(met0, handled0, pred_turned[:, 0:P], "0")
        back = psum.tile([P, S], F32, name="back", tag="y0_0")
        nc.tensor.transpose(back[:, 0:P], res_turned[:], identity[:])
        res0 = keep.tile([P, V], F32, name="res0_sb")
        nc.scalar.copy(res0[:], back[:, 0:P])
        nc.sync.dma_start(out[0:P, :], res0[:])

        pairs = [keep.tile([P, V, 2], F32, name="pairs%d" % i) for i in range(2)]
        sums = [keep.tile([P, V], F32, name="sums%d" % i) for i in range(2)]
        for i, terms in enumerate((gh1, enc1)):
            four = terms[:].rearrange("p (v d) -> p v d", d=D)
            nc.vector.tensor_tensor(pairs[i][:], four[:, :, 0:2], four[:, :, 2:4], ALU.add)
        for i in range(2):
            nc.vector.tensor_tensor(sums[i][:], pairs[i][:, :, 0], pairs[i][:, :, 1], ALU.add)

        res1 = growth(sums[1][:], sums[0][:], pred_sb[:, 1, :], "1")
        nc.sync.dma_start(out[P : 2 * P, :], res1[:])
